import numpy as np
import ml_dtypes


def mxq(x, axis, fmt="e4m3"):
    dtype, down = {"e4m3": (ml_dtypes.float8_e4m3fn, 7), "e5m2": (ml_dtypes.float8_e5m2, 14)}[fmt]
    v = np.moveaxis(np.asarray(x, np.float32).astype(ml_dtypes.bfloat16).astype(np.float64), axis, -1)
    blocks = v.reshape(v.shape[:-1] + (-1, 32))
    amax = np.abs(blocks).max(-1, keepdims=True)
    byte = np.maximum(np.where(amax > 0, np.frexp(amax)[1] - 1 + 127, 0) - down, 1)
    scale = np.exp2(byte - 127.0)
    codes = (blocks / scale).astype(np.float32).astype(dtype).astype(np.float64)
    return np.moveaxis((codes * scale).reshape(v.shape), -1, axis)


WIDE = False


def mx_kscale(k, group=512):
    if not WIDE:
        return np.ones(k)
    levels = np.array([10, -10, 5, -5, 0])
    if group != 512:
        return np.exp2(np.random.permutation(np.resize(levels, k // group))).repeat(group)
    if k % 512:
        return np.exp2(np.random.permutation(np.resize(levels, k // 32))).repeat(32)
    a = np.empty((k // 512, 16))
    for p in range(k // 512):
        a[p, :8] = np.random.permutation(np.resize(levels, 8))
        for g in range(8):
            far = levels[np.abs(levels - a[p, g]) >= 10]
            a[p, g + 8] = far[np.random.randint(len(far))]
    return np.exp2(a.ravel()).repeat(32)


def f64(x):
    return np.asarray(x).astype(np.float64)


def striped(idx):
    return np.tile(np.asarray(idx).reshape(-1, 16).T, (8, 1)).astype(np.uint16)


def unstriped(offs):
    return offs[:16].T.reshape(-1).astype(np.int64)


H, KV, D, NQ, N = 4, 4, 128, 512, 512


def setup_inputs():
    n = np.random.standard_normal
    s = mx_kscale(D, 0)[:, None]
    u = mx_kscale(N)
    t = np.random.uniform(0.5, 2.0, N) * u
    v = n((KV, N, 128))
    return {
        "qT": (n((H, D, NQ)) * s * (0.70 / np.sqrt(D))).astype(np.float32),
        "kT": (n((KV, D, N)) / s).astype(np.float32),
        "t": t.reshape(N, 1).astype(np.float32),
        "v": (v / t[:, None]).astype(np.float32),
        "gn": np.tile(np.random.uniform(0.5, 2.0, 128), (128, 1)).astype(np.float32),
    }


def reference(qT, kT, t, v, gn):
    a = mxq(f64(kT), 1, "e4m3").transpose(0, 2, 1) @ mxq(f64(qT), 1, "e4m3")
    p = np.maximum(a, 0.0)
    w = p * f64(t)
    y = mxq(w, 1, "e4m3").transpose(0, 2, 1) @ mxq(f64(v), 1, "e4m3")
    y = y / 16.0
    y = y / np.sqrt(np.mean(np.square(y), -1, keepdims=True) + 1e-5) * f64(gn)[:1]
    return y

@@ -1,0 +1,289 @@
+from contextlib import ExitStack
+
+import concourse.mybir as mybir
+
+F32 = mybir.dt.float32
+BF16 = mybir.dt.bfloat16
+U32 = mybir.dt.uint32
+U8 = mybir.dt.uint8
+FP8X4 = mybir.dt.float8_e4m3fn_x4
+ACT = mybir.ActivationFunctionType
+ALU = mybir.AluOpType
+
+H, D, NQ, N, E = 4, 128, 512, 512, 128
+P = 128
+PACK = 4
+ROWS = D // PACK
+QT = 128
+TILES = NQ // QT
+FLOPS = 2 * H * NQ * N * (D + E)
+
+
+def tile_rows_a_relu_onorm_kernel(tc, qT, kT, t, v, gn, out):
+    nc = tc.nc
+    with ExitStack() as ctx:
+        sb = ctx.enter_context(tc.tile_pool(name="sb", bufs=1))
+        ps = ctx.enter_context(tc.psum_pool(name="ps", bufs=1))
+        ctx.enter_context(tc.manual_schedule())
+
+        def tiles(name, count, shape, dtype):
+            return [sb.tile(shape, dtype, name="%s%d" % (name, i), align_bytes=64) for i in range(count)]
+
+        k_raw = sb.tile([P, PACK, N], F32)
+        q_raw0 = sb.tile([P, PACK, QT], F32)
+        q_raw1 = sb.tile([P, PACK, NQ - QT], F32)
+        v_raw = tiles("v_raw", 2, [P, 2, PACK, E], F32)
+        t_sb = sb.tile([P, PACK], F32)
+        gn_sb = sb.tile([P, E], F32)
+
+        k_bf = tiles("k_bf", 2, [P, 2, P, PACK], BF16)
+        k_codes = tiles("k_codes", 2, [P, 2 * P], U32)
+        k_scales = tiles("k_scales", 2, [P, 2 * P], U8)
+        q_widths = [QT, QT, 2 * QT]
+        q_bf = [sb.tile([P, w, PACK], BF16, name="q_bf%d" % i, align_bytes=64) for i, w in enumerate(q_widths)]
+        q_codes = [sb.tile([P, w], U32, name="q_codes%d" % i, align_bytes=64) for i, w in enumerate(q_widths)]
+        q_scales = [sb.tile([P, w], U8, name="q_scales%d" % i, align_bytes=64) for i, w in enumerate(q_widths)]
+        v_bf = tiles("v_bf", 2, [P, 2, E, PACK], BF16)
+        v_codes = tiles("v_codes", 2, [P, 2 * E], U32)
+        v_scales = tiles("v_scales", 2, [P, 2 * E], U8)
+        w_bf = tiles("w_bf", TILES, [P, H * QT * PACK], BF16)
+        w_codes = tiles("w_codes", TILES, [P, H * QT], U32)
+        w_scales = tiles("w_scales", TILES, [P, H * QT], U8)
+        relu_sb = tiles("relu_sb", TILES, [P, 2, QT * PACK], F32)
+        squares = tiles("squares", TILES, [P, H, E], BF16)
+        sums = tiles("sums", TILES, [P, H], F32)
+        inv = tiles("inv", TILES, [P, H], F32)
+        res = tiles("res", TILES, [P, H, E], F32)
+        score = [ps.tile([P, PACK, QT], F32, name="score%d" % g) for g in range(H)]
+        y = [ps.tile([P, E], F32, name="y%d" % g) for g in range(H)]
+
+        q_view = qT.rearrange("h (p j) n -> (h p) j n", j=PACK)
+        k_view = kT.rearrange("h (p j) n -> (h p) j n", j=PACK)
+        v_view = v.rearrange("h (p j) e -> p h (j e)", j=PACK)
+        out_view = out.rearrange("h q e -> q h e")
+
+        def quantize(codes, scales, src):
+            nc.vector.quantize_mx(out=codes.bitcast(FP8X4), scales=scales, in_=src)
+
+        def load_k():
+            nc.sync.dma_start(out=k_raw[:], in_=k_view)
+
+        def load_q0():
+            nc.sync.dma_start(out=q_raw0[:], in_=q_view[:, :, 0:QT])
+
+        def load_q1():
+            nc.sync.dma_start(out=q_raw1[:], in_=q_view[:, :, QT:NQ])
+
+        def load_t():
+            nc.sync.dma_start(out=t_sb[:], in_=t.rearrange("(p j) o -> p (j o)", j=PACK))
+
+        def load_v(i):
+            nc.sync.dma_start(out=v_raw[i][:].rearrange("p h j e -> p h (j e)"), in_=v_view[:, 2 * i : 2 * i + 2, :])
+
+        def load_gn():
+            nc.sync.dma_start(out=gn_sb[:], in_=gn)
+
+        def warm():
+            one = sb.tile([P, 1], F32)
+            warm_out = sb.tile([P, 1], F32)
+            nc.gpsimd.memset(one[:], 1.0)
+            nc.scalar.activation(out=warm_out[:], in_=one[:], func=ACT.Abs_reciprocal_sqrt)
+
+        def cast_k(copy, i):
+            src = k_raw[:].rearrange("p j (s r) -> p s j r", r=PACK)[:, :, :, 2 * i : 2 * i + 2]
+            copy(out=k_bf[i][:].rearrange("p r s j -> p s j r"), in_=src)
+
+        def quant_k(i):
+            quantize(k_codes[i][:], k_scales[i][:], k_bf[i][:].rearrange("p r s j -> p (r s j)"))
+
+        def cast_q(copy, i):
+            raw = [q_raw0[:], q_raw1[:, :, 0:QT], q_raw1[:, :, QT : 3 * QT]][i]
+            copy(
+                out=q_bf[i][:].rearrange("p (c i) j -> p c j i", i=PACK),
+                in_=raw.rearrange("p j (c i) -> p c j i", i=PACK),
+            )
+
+        def quant_q(i):
+            quantize(q_codes[i][:], q_scales[i][:], q_bf[i][:].rearrange("p n j -> p (n j)"))
+
+        def cast_v(copy, i):
+            copy(
+                out=v_bf[i][:].rearrange("p h (c i) j -> p h c j i", i=PACK),
+                in_=v_raw[i][:].rearrange("p h j (c i) -> p h c j i", i=PACK),
+            )
+
+        def quant_v(i):
+            quantize(v_codes[i][:], v_scales[i][:], v_bf[i][:].rearrange("p h e j -> p (h e j)"))
+
+        def scores(c, g):
+            rows = slice(ROWS * g, ROWS * (g + 1))
+            piece = min(c, 2)
+            q_cols = slice(QT * (c - piece), QT * (c - piece + 1))
+            for r in range(PACK):
+                k_cols = slice(P * (r % 2), P * (r % 2 + 1))
+                nc.tensor.matmul_mx(
+                    out=score[g][:, r, :],
+                    lhsT=k_codes[r // 2][rows, k_cols].bitcast(FP8X4),
+                    lhsT_scale=k_scales[r // 2][rows, k_cols],
+                    rhs=q_codes[piece][rows, q_cols].bitcast(FP8X4),
+                    rhs_scale=q_scales[piece][rows, q_cols],
+                    start=True,
+                    stop=True,
+                )
+
+        def w_slot(c, g):
+            return w_bf[c][:, g * QT * PACK : (g + 1) * QT * PACK].rearrange("p (q r) -> p q r", r=PACK)
+
+        t_wide = t_sb[:, 0:PACK].unsqueeze(1).to_broadcast([P, QT, PACK])
+
+        def weigh(c, g):
+            nc.vector.scalar_tensor_tensor(
+                out=w_slot(c, g),
+                in0=score[g][:].rearrange("p r q -> p q r"),
+                scalar=0.0,
+                in1=t_wide,
+                op0=ALU.max,
+                op1=ALU.mult,
+            )
+
+        def relu(c, g, slot):
+            nc.scalar.activation(
+                out=relu_sb[c][:, slot, :].rearrange("p (q r) -> p q r", r=PACK),
+                in_=score[g][:].rearrange("p r q -> p q r"),
+                func=ACT.Relu,
+            )
+
+        def scale_w(c, g, slot):
+            nc.gpsimd.tensor_tensor(
+                out=w_slot(c, g),
+                in0=relu_sb[c][:, slot, :].rearrange("p (q r) -> p q r", r=PACK),
+                in1=t_wide,
+                op=ALU.mult,
+            )
+
+        def quant_w(c, g0, g1):
+            quantize(
+                w_codes[c][:, g0 * QT : g1 * QT],
+                w_scales[c][:, g0 * QT : g1 * QT],
+                w_bf[c][:, g0 * QT * PACK : g1 * QT * PACK],
+            )
+
+        def values(c, g):
+            w_cols = slice(g * QT, (g + 1) * QT)
+            v_cols = slice((g % 2) * E, (g % 2 + 1) * E)
+            nc.tensor.matmul_mx(
+                out=y[g][:],
+                lhsT=w_codes[c][:, w_cols].bitcast(FP8X4),
+                lhsT_scale=w_scales[c][:, w_cols],
+                rhs=v_codes[g // 2][:, v_cols].bitcast(FP8X4),
+                rhs_scale=v_scales[g // 2][:, v_cols],
+                start=True,
+                stop=True,
+            )
+
+        def square(c, g):
+            nc.scalar.activation(
+                out=squares[c][:, g, :], in_=y[g][:], func=ACT.Square, accum_out=sums[c][:, g : g + 1]
+            )
+
+        def root(c, g0, g1):
+            nc.scalar.activation(
+                out=inv[c][:, g0:g1],
+                in_=sums[c][:, g0:g1],
+                func=ACT.Abs_reciprocal_sqrt,
+                scale=1.0 / E,
+                bias=256.0 * 1e-5,
+            )
+
+        def finish(c, g):
+            nc.vector.scalar_tensor_tensor(
+                out=res[c][:, g, :],
+                in0=y[g][:],
+                scalar=inv[c][:, g : g + 1],
+                in1=gn_sb[:],
+                op0=ALU.mult,
+                op1=ALU.mult,
+            )
+
+        def store(c, g0, g1):
+            nc.sync.dma_start(out=out_view[c * QT : (c + 1) * QT, g0:g1, :], in_=res[c][:, g0:g1, :])
+
+        def norm(c, g0, g1):
+            for g in range(g0, g1):
+                values(c, g)
+                square(c, g)
+            root(c, g0, g1)
+
+        def done(c, g0, g1):
+            for g in range(g0, g1):
+                finish(c, g)
+            store(c, g0, g1)
+
+        vcopy = nc.vector.tensor_copy
+        scopy = nc.scalar.copy
+
+        load_k()
+        load_q0()
+        load_t()
+        load_q1()
+        load_v(0)
+        load_v(1)
+        load_gn()
+        warm()
+        cast_k(vcopy, 0)
+        cast_k(scopy, 1)
+        quant_k(0)
+        cast_q(vcopy, 0)
+        quant_k(1)
+        quant_q(0)
+        cast_q(scopy, 1)
+        cast_q(scopy, 2)
+        cast_v(scopy, 0)
+        cast_v(scopy, 1)
+        for g in range(H):
+            scores(0, g)
+        weigh(0, 0)
+        quant_q(1)
+        scores(1, 0)
+        for g in range(1, H):
+            weigh(0, g)
+            scores(1, g)
+        weigh(1, 0)
+        quant_w(0, 0, 4)
+        quant_q(2)
+        scores(2, 0)
+        weigh(1, 1)
+        quant_v(0)
+        scores(2, 1)
+        weigh(1, 2)
+        scores(2, 2)
+        weigh(1, 3)
+        scores(2, 3)
+        quant_v(1)
+        norm(0, 0, 4)
+        weigh(2, 0)
+        scores(3, 0)
+        quant_w(1, 0, 4)
+        weigh(2, 1)
+        scores(3, 1)
+        done(0, 0, 4)
+        norm(1, 0, 4)
+        weigh(2, 2)
+        scores(3, 2)
+        weigh(2, 3)
+        scores(3, 3)
+        weigh(3, 0)
+        quant_w(2, 0, 4)
+        done(1, 0, 4)
+        norm(2, 0, 4)
+        weigh(3, 1)
+        weigh(3, 2)
+        quant_w(3, 0, 2)
+        done(2, 0, 2)
+        norm(3, 0, 2)
+        weigh(3, 3)
+        done(2, 2, 4)
+        quant_w(3, 2, 4)
+        norm(3, 2, 4)
+        done(3, 0, 2)
+        done(3, 2, 4)

@@ -30,8 +30,8 @@ def tile_rows_a_relu_onorm_kernel(tc, qT, kT, t, v, gn, out):
             return [sb.tile(shape, dtype, name="%s%d" % (name, i), align_bytes=64) for i in range(count)]
 
         k_raw = sb.tile([P, PACK, N], F32)
-        q_raw0 = sb.tile([P, PACK, QT], F32)
-        q_raw1 = sb.tile([P, PACK, NQ - QT], F32)
+        q_raw0 = sb.tile([P, PACK, 2 * QT], F32)
+        q_raw1 = sb.tile([P, PACK, 2 * QT], F32)
         v_raw = tiles("v_raw", 2, [P, 2, PACK, E], F32)
         t_sb = sb.tile([P, PACK], F32)
         gn_sb = sb.tile([P, E], F32)
@@ -46,16 +46,36 @@ def tile_rows_a_relu_onorm_kernel(tc, qT, kT, t, v, gn, out):
         v_bf = tiles("v_bf", 2, [P, 2, E, PACK], BF16)
         v_codes = tiles("v_codes", 2, [P, 2 * E], U32)
         v_scales = tiles("v_scales", 2, [P, 2 * E], U8)
-        w_bf = tiles("w_bf", TILES, [P, H * QT * PACK], BF16)
+        w_bf = {}
+        w_plan = [[(0, 4, "slot_a")], [(0, 2, "w1"), (2, 4, "slot_a")], [(0, 4, "slot_b")], [(0, 4, "w3")]]
+        res_tags = ["slot_a", "slot_b", "res2", "res3"]
+        res = {}
+        scaled = tiles("scaled", TILES, [P, H, E], F32)
         w_codes = tiles("w_codes", TILES, [P, H * QT], U32)
         w_scales = tiles("w_scales", TILES, [P, H * QT], U8)
         relu_sb = tiles("relu_sb", TILES, [P, 2, QT * PACK], F32)
         squares = tiles("squares", TILES, [P, H, E], BF16)
         sums = tiles("sums", TILES, [P, H], F32)
         inv = tiles("inv", TILES, [P, H], F32)
-        res = tiles("res", TILES, [P, H, E], F32)
         score = [ps.tile([P, PACK, QT], F32, name="score%d" % g) for g in range(H)]
-        y = [ps.tile([P, E], F32, name="y%d" % g) for g in range(H)]
+        y_banks = [ps.tile([P, H, E], F32, name="y%d" % g) for g in range(TILES)]
+
+        def y(c, g):
+            bank = c if c < TILES - 1 else [c, c, 0, 1][g]
+            return y_banks[bank][:, g, :]
+
+        def w_cols(c, g0, g1):
+            for first, last, tag in w_plan[c]:
+                if first <= g0 and g1 <= last:
+                    if (c, first) not in w_bf:
+                        w_bf.setdefault((c, first), sb.tile([P, (last - first) * QT * PACK], BF16, name="w_%d_%d" % (c, first), tag=tag, align_bytes=64))
+                    return w_bf[(c, first)][:, (g0 - first) * QT * PACK : (g1 - first) * QT * PACK]
+            raise ValueError("no such piece")
+
+        def result(c):
+            if c not in res:
+                res.setdefault(c, sb.tile([P, H, E], F32, name="res%d" % c, tag=res_tags[c], align_bytes=64))
+            return res[c]
 
         q_view = qT.rearrange("h (p j) n -> (h p) j n", j=PACK)
         k_view = kT.rearrange("h (p j) n -> (h p) j n", j=PACK)
@@ -68,11 +88,11 @@ def tile_rows_a_relu_onorm_kernel(tc, qT, kT, t, v, gn, out):
         def load_k():
             nc.sync.dma_start(out=k_raw[:], in_=k_view)
 
-        def load_q0():
-            nc.sync.dma_start(out=q_raw0[:], in_=q_view[:, :, 0:QT])
+        def load_qa():
+            nc.sync.dma_start(out=q_raw0[:], in_=q_view[:, :, 0 : 2 * QT])
 
-        def load_q1():
-            nc.sync.dma_start(out=q_raw1[:], in_=q_view[:, :, QT:NQ])
+        def load_qb():
+            nc.sync.dma_start(out=q_raw1[:], in_=q_view[:, :, 2 * QT : NQ])
 
         def load_t():
             nc.sync.dma_start(out=t_sb[:], in_=t.rearrange("(p j) o -> p (j o)", j=PACK))
@@ -97,7 +117,7 @@ def tile_rows_a_relu_onorm_kernel(tc, qT, kT, t, v, gn, out):
             quantize(k_codes[i][:], k_scales[i][:], k_bf[i][:].rearrange("p r s j -> p (r s j)"))
 
         def cast_q(copy, i):
-            raw = [q_raw0[:], q_raw1[:, :, 0:QT], q_raw1[:, :, QT : 3 * QT]][i]
+            raw = [q_raw0[:, :, 0:QT], q_raw0[:, :, QT : 2 * QT], q_raw1[:]][i]
             copy(
                 out=q_bf[i][:].rearrange("p (c i) j -> p c j i", i=PACK),
                 in_=raw.rearrange("p j (c i) -> p c j i", i=PACK),
@@ -132,7 +152,7 @@ def tile_rows_a_relu_onorm_kernel(tc, qT, kT, t, v, gn, out):
                 )
 
         def w_slot(c, g):
-            return w_bf[c][:, g * QT * PACK : (g + 1) * QT * PACK].rearrange("p (q r) -> p q r", r=PACK)
+            return w_cols(c, g, g + 1).rearrange("p (q r) -> p q r", r=PACK)
 
         t_wide = t_sb[:, 0:PACK].unsqueeze(1).to_broadcast([P, QT, PACK])
 
@@ -165,16 +185,16 @@ def tile_rows_a_relu_onorm_kernel(tc, qT, kT, t, v, gn, out):
             quantize(
                 w_codes[c][:, g0 * QT : g1 * QT],
                 w_scales[c][:, g0 * QT : g1 * QT],
-                w_bf[c][:, g0 * QT * PACK : g1 * QT * PACK],
+                w_cols(c, g0, g1),
             )
 
-        def values(c, g):
-            w_cols = slice(g * QT, (g + 1) * QT)
+        def value(c, g):
+            w_span = slice(g * QT, (g + 1) * QT)
             v_cols = slice((g % 2) * E, (g % 2 + 1) * E)
             nc.tensor.matmul_mx(
-                out=y[g][:],
-                lhsT=w_codes[c][:, w_cols].bitcast(FP8X4),
-                lhsT_scale=w_scales[c][:, w_cols],
+                out=y(c, g),
+                lhsT=w_codes[c][:, w_span].bitcast(FP8X4),
+                lhsT_scale=w_scales[c][:, w_span],
                 rhs=v_codes[g // 2][:, v_cols].bitcast(FP8X4),
                 rhs_scale=v_scales[g // 2][:, v_cols],
                 start=True,
@@ -183,7 +203,7 @@ def tile_rows_a_relu_onorm_kernel(tc, qT, kT, t, v, gn, out):
 
         def square(c, g):
             nc.scalar.activation(
-                out=squares[c][:, g, :], in_=y[g][:], func=ACT.Square, accum_out=sums[c][:, g : g + 1]
+                out=squares[c][:, g, :], in_=y(c, g), func=ACT.Square, accum_out=sums[c][:, g : g + 1]
             )
 
         def root(c, g0, g1):
@@ -195,10 +215,10 @@ def tile_rows_a_relu_onorm_kernel(tc, qT, kT, t, v, gn, out):
                 bias=256.0 * 1e-5,
             )
 
-        def finish(c, g):
+        def finish_one(c, g):
             nc.vector.scalar_tensor_tensor(
-                out=res[c][:, g, :],
-                in0=y[g][:],
+                out=result(c)[:, g, :],
+                in0=y(c, g),
                 scalar=inv[c][:, g : g + 1],
                 in1=gn_sb[:],
                 op0=ALU.mult,
@@ -206,28 +226,42 @@ def tile_rows_a_relu_onorm_kernel(tc, qT, kT, t, v, gn, out):
             )
 
         def store(c, g0, g1):
-            nc.sync.dma_start(out=out_view[c * QT : (c + 1) * QT, g0:g1, :], in_=res[c][:, g0:g1, :])
+            nc.sync.dma_start(out=out_view[c * QT : (c + 1) * QT, g0:g1, :], in_=result(c)[:, g0:g1, :])
+
+        def values(c, g0, g1):
+            for g in range(g0, g1):
+                value(c, g)
+
+        def rescale(c, g0, g1):
+            for g in range(g0, g1):
+                nc.scalar.activation(out=scaled[c][:, g, :], in_=y(c, g), func=ACT.Copy, scale=inv[c][:, g : g + 1])
+
+        def gain(c, g0, g1):
+            nc.gpsimd.tensor_tensor(
+                out=result(c)[:, g0:g1, :],
+                in0=scaled[c][:, g0:g1, :],
+                in1=gn_sb[:].unsqueeze(1).to_broadcast([P, g1 - g0, E]),
+                op=ALU.mult,
+            )
 
         def norm(c, g0, g1):
             for g in range(g0, g1):
-                values(c, g)
                 square(c, g)
             root(c, g0, g1)
 
-        def done(c, g0, g1):
+        def finish(c, g0, g1):
             for g in range(g0, g1):
-                finish(c, g)
-            store(c, g0, g1)
+                finish_one(c, g)
 
         vcopy = nc.vector.tensor_copy
         scopy = nc.scalar.copy
 
         load_k()
-        load_q0()
+        load_qa()
         load_t()
-        load_q1()
         load_v(0)
         load_v(1)
+        load_qb()
         load_gn()
         warm()
         cast_k(vcopy, 0)
@@ -235,55 +269,77 @@ def tile_rows_a_relu_onorm_kernel(tc, qT, kT, t, v, gn, out):
         quant_k(0)
         cast_q(vcopy, 0)
         quant_k(1)
-        quant_q(0)
         cast_q(scopy, 1)
-        cast_q(scopy, 2)
-        cast_v(scopy, 0)
-        cast_v(scopy, 1)
-        for g in range(H):
-            scores(0, g)
-        weigh(0, 0)
+        quant_q(0)
+        scores(0, 0)
+        scores(0, 1)
+        scores(0, 2)
+        scores(0, 3)
         quant_q(1)
+        cast_v(scopy, 0)
+        weigh(0, 0)
         scores(1, 0)
-        for g in range(1, H):
-            weigh(0, g)
-            scores(1, g)
+        relu(0, 3, 0)
+        scale_w(0, 3, 0)
+        scores(1, 3)
+        weigh(0, 1)
+        scores(1, 1)
+        weigh(0, 2)
+        scores(1, 2)
+        cast_v(scopy, 1)
+        cast_q(scopy, 2)
+        relu(1, 3, 0)
         weigh(1, 0)
-        quant_w(0, 0, 4)
-        quant_q(2)
-        scores(2, 0)
         weigh(1, 1)
         quant_v(0)
+        quant_v(1)
+        quant_q(2)
+        scores(2, 0)
         scores(2, 1)
+        scores(2, 3)
+        quant_w(0, 0, 4)
+        values(0, 0, 4)
+        scale_w(1, 3, 0)
+        norm(0, 0, 4)
+        rescale(0, 0, 4)
         weigh(1, 2)
         scores(2, 2)
-        weigh(1, 3)
-        scores(2, 3)
-        quant_v(1)
-        norm(0, 0, 4)
         weigh(2, 0)
         scores(3, 0)
-        quant_w(1, 0, 4)
+        quant_w(1, 0, 2)
+        quant_w(1, 2, 4)
+        values(1, 0, 4)
+        gain(0, 0, 4)
+        store(0, 0, 4)
+        norm(1, 0, 4)
+        rescale(1, 0, 4)
         weigh(2, 1)
         scores(3, 1)
-        done(0, 0, 4)
-        norm(1, 0, 4)
         weigh(2, 2)
         scores(3, 2)
         weigh(2, 3)
         scores(3, 3)
         weigh(3, 0)
         quant_w(2, 0, 4)
-        done(1, 0, 4)
+        values(2, 0, 4)
+        gain(1, 0, 4)
+        store(1, 0, 4)
         norm(2, 0, 4)
         weigh(3, 1)
         weigh(3, 2)
         quant_w(3, 0, 2)
-        done(2, 0, 2)
+        values(3, 0, 2)
         norm(3, 0, 2)
         weigh(3, 3)
-        done(2, 2, 4)
-        quant_w(3, 2, 4)
-        norm(3, 2, 4)
-        done(3, 0, 2)
-        done(3, 2, 4)
+        quant_w(3, 2, 3)
+        values(3, 2, 3)
+        quant_w(3, 3, 4)
+        values(3, 3, 4)
+        norm(3, 2, 3)
+        norm(3, 3, 4)
+        finish(2, 0, 4)
+        store(2, 0, 4)
+        finish(3, 0, 2)
+        store(3, 0, 2)
+        finish(3, 2, 4)
+        store(3, 2, 4)

@@ -40,14 +40,14 @@ def tile_rows_a_relu_onorm_kernel(tc, qT, kT, t, v, gn, out):
         k_codes = tiles("k_codes", 2, [P, 2 * P], U32)
         k_scales = tiles("k_scales", 2, [P, 2 * P], U8)
         q_widths = [QT, QT, 2 * QT]
-        q_bf = [sb.tile([P, w, PACK], BF16, name="q_bf%d" % i, align_bytes=64) for i, w in enumerate(q_widths)]
         q_codes = [sb.tile([P, w], U32, name="q_codes%d" % i, align_bytes=64) for i, w in enumerate(q_widths)]
         q_scales = [sb.tile([P, w], U8, name="q_scales%d" % i, align_bytes=64) for i, w in enumerate(q_widths)]
-        v_bf = tiles("v_bf", 2, [P, 2, E, PACK], BF16)
-        v_codes = tiles("v_codes", 2, [P, 2 * E], U32)
-        v_scales = tiles("v_scales", 2, [P, 2 * E], U8)
+        q_bf0 = sb.tile([P, QT * PACK], BF16, align_bytes=64)
+        v_bf = sb.tile([P, H * E * PACK], BF16, align_bytes=64)
+        v_codes = sb.tile([P, H * E], U32, align_bytes=64)
+        v_scales = sb.tile([P, H * E], U8, align_bytes=64)
         w_bf = {}
-        w_plan = [[(0, 4, "slot_a")], [(0, 2, "w1"), (2, 4, "slot_a")], [(0, 4, "slot_b")], [(0, 4, "w3")]]
+        w_plan = [[(0, 4, "w0")], [(0, 4, "slot_a")], [(0, 4, "w2")], [(0, 2, "slot_b"), (2, 4, "w3")]]
         res_tags = ["slot_a", "slot_b", "res2", "res3"]
         res = {}
         scaled = tiles("scaled", TILES, [P, H, E], F32)
@@ -61,7 +61,7 @@ def tile_rows_a_relu_onorm_kernel(tc, qT, kT, t, v, gn, out):
         y_banks = [ps.tile([P, H, E], F32, name="y%d" % g) for g in range(TILES)]
 
         def y(c, g):
-            bank = c if c < TILES - 1 else [c, c, 0, 1][g]
+            bank = (2 * c + g // 2) % TILES
             return y_banks[bank][:, g, :]
 
         def w_cols(c, g0, g1):
@@ -77,6 +77,7 @@ def tile_rows_a_relu_onorm_kernel(tc, qT, kT, t, v, gn, out):
                 res.setdefault(c, sb.tile([P, H, E], F32, name="res%d" % c, tag=res_tags[c], align_bytes=64))
             return res[c]
 
+        q_bf = [q_bf0[:], v_bf[:, 0 : QT * PACK], w_cols(1, 2, 4)]
         q_view = qT.rearrange("h (p j) n -> (h p) j n", j=PACK)
         k_view = kT.rearrange("h (p j) n -> (h p) j n", j=PACK)
         v_view = v.rearrange("h (p j) e -> p h (j e)", j=PACK)
@@ -109,37 +110,48 @@ def tile_rows_a_relu_onorm_kernel(tc, qT, kT, t, v, gn, out):
             nc.gpsimd.memset(one[:], 1.0)
             nc.scalar.activation(out=warm_out[:], in_=one[:], func=ACT.Abs_reciprocal_sqrt)
 
-        def cast_k(copy, i):
-            src = k_raw[:].rearrange("p j (s r) -> p s j r", r=PACK)[:, :, :, 2 * i : 2 * i + 2]
-            copy(out=k_bf[i][:].rearrange("p r s j -> p s j r"), in_=src)
+        def gcopy(out, in_):
+            nc.gpsimd.tensor_scalar(out=out, in0=in_, scalar1=1.0, scalar2=0.0, op0=ALU.mult, op1=ALU.add)
 
-        def quant_k(i):
+        def cast_kp(copy, i, s0, s1):
+            src = k_raw[:].rearrange("p j (s r) -> p s j r", r=PACK)[:, s0:s1, :, 2 * i : 2 * i + 2]
+            copy(out=k_bf[i][:].rearrange("p r s j -> p s j r")[:, s0:s1, :, :], in_=src)
+
+        def quant_kp(i):
             quantize(k_codes[i][:], k_scales[i][:], k_bf[i][:].rearrange("p r s j -> p (r s j)"))
 
-        def cast_q(copy, i):
+        def cast_qp(copy, i, n0, n1):
             raw = [q_raw0[:, :, 0:QT], q_raw0[:, :, QT : 2 * QT], q_raw1[:]][i]
             copy(
-                out=q_bf[i][:].rearrange("p (c i) j -> p c j i", i=PACK),
-                in_=raw.rearrange("p j (c i) -> p c j i", i=PACK),
+                out=q_bf[i][:, n0 * PACK : n1 * PACK].rearrange("p (c i j) -> p c j i", i=PACK, j=PACK),
+                in_=raw[:, :, n0:n1].rearrange("p j (c i) -> p c j i", i=PACK),
             )
 
-        def quant_q(i):
-            quantize(q_codes[i][:], q_scales[i][:], q_bf[i][:].rearrange("p n j -> p (n j)"))
+        def quant_qp(i):
+            quantize(q_codes[i][:], q_scales[i][:], q_bf[i])
 
         def cast_v(copy, i):
-            copy(
-                out=v_bf[i][:].rearrange("p h (c i) j -> p h c j i", i=PACK),
-                in_=v_raw[i][:].rearrange("p h j (c i) -> p h c j i", i=PACK),
-            )
+            half = v_bf[:, i * 2 * E * PACK : (i + 1) * 2 * E * PACK]
+            if copy is gcopy:
+                copy(out=half.rearrange("p (h e j) -> p h e j", h=2, j=PACK), in_=v_raw[i][:].rearrange("p h j e -> p h e j"))
+            else:
+                copy(
+                    out=half.rearrange("p (h c i j) -> p h c j i", h=2, i=PACK, j=PACK),
+                    in_=v_raw[i][:].rearrange("p h j (c i) -> p h c j i", i=PACK),
+                )
 
-        def quant_v(i):
-            quantize(v_codes[i][:], v_scales[i][:], v_bf[i][:].rearrange("p h e j -> p (h e j)"))
+        def quant_v_all():
+            quantize(v_codes[:], v_scales[:], v_bf[:])
 
         def scores(c, g):
+            scores_half(c, g, 0)
+            scores_half(c, g, 1)
+
+        def scores_half(c, g, half):
             rows = slice(ROWS * g, ROWS * (g + 1))
             piece = min(c, 2)
             q_cols = slice(QT * (c - piece), QT * (c - piece + 1))
-            for r in range(PACK):
+            for r in range(2 * half, 2 * half + 2):
                 k_cols = slice(P * (r % 2), P * (r % 2 + 1))
                 nc.tensor.matmul_mx(
                     out=score[g][:, r, :],
@@ -190,13 +202,13 @@ def tile_rows_a_relu_onorm_kernel(tc, qT, kT, t, v, gn, out):
 
         def value(c, g):
             w_span = slice(g * QT, (g + 1) * QT)
-            v_cols = slice((g % 2) * E, (g % 2 + 1) * E)
+            v_cols = slice(g * E, (g + 1) * E)
             nc.tensor.matmul_mx(
                 out=y(c, g),
                 lhsT=w_codes[c][:, w_span].bitcast(FP8X4),
                 lhsT_scale=w_scales[c][:, w_span],
-                rhs=v_codes[g // 2][:, v_cols].bitcast(FP8X4),
-                rhs_scale=v_scales[g // 2][:, v_cols],
+                rhs=v_codes[:, v_cols].bitcast(FP8X4),
+                rhs_scale=v_scales[:, v_cols],
                 start=True,
                 stop=True,
             )
@@ -264,79 +276,81 @@ def tile_rows_a_relu_onorm_kernel(tc, qT, kT, t, v, gn, out):
         load_qb()
         load_gn()
         warm()
-        cast_k(vcopy, 0)
-        cast_k(scopy, 1)
-        quant_k(0)
-        cast_q(vcopy, 0)
-        quant_k(1)
-        cast_q(scopy, 1)
-        quant_q(0)
-        scores(0, 0)
+        cast_kp(vcopy, 0, 0, 128)
+        cast_kp(vcopy, 1, 0, 32)
+        cast_kp(scopy, 1, 32, 128)
+        quant_kp(0)
+        cast_qp(vcopy, 0, 0, 64)
+        cast_qp(scopy, 0, 64, 128)
+        quant_qp(0)
+        scores_half(0, 0, 0)
+        scores_half(0, 3, 0)
+        quant_kp(1)
+        scores_half(0, 0, 1)
+        scores_half(0, 3, 1)
         scores(0, 1)
         scores(0, 2)
-        scores(0, 3)
-        quant_q(1)
-        cast_v(scopy, 0)
+        cast_qp(scopy, 1, 0, 128)
+        quant_qp(1)
+        cast_v(gcopy, 0)
         weigh(0, 0)
         scores(1, 0)
         relu(0, 3, 0)
-        scale_w(0, 3, 0)
         scores(1, 3)
+        scale_w(0, 3, 0)
         weigh(0, 1)
         scores(1, 1)
         weigh(0, 2)
         scores(1, 2)
         cast_v(scopy, 1)
-        cast_q(scopy, 2)
+        cast_qp(scopy, 2, 0, 256)
         relu(1, 3, 0)
         weigh(1, 0)
-        weigh(1, 1)
-        quant_v(0)
-        quant_v(1)
-        quant_q(2)
-        scores(2, 0)
-        scores(2, 1)
-        scores(2, 3)
+        quant_v_all()
         quant_w(0, 0, 4)
         values(0, 0, 4)
+        quant_qp(2)
+        scores(2, 0)
+        scores(2, 3)
         scale_w(1, 3, 0)
         norm(0, 0, 4)
         rescale(0, 0, 4)
+        weigh(1, 1)
+        scores(2, 1)
         weigh(1, 2)
         scores(2, 2)
         weigh(2, 0)
         scores(3, 0)
-        quant_w(1, 0, 2)
-        quant_w(1, 2, 4)
+        quant_w(1, 0, 4)
         values(1, 0, 4)
         gain(0, 0, 4)
         store(0, 0, 4)
+        relu(2, 3, 0)
+        scores(3, 3)
+        scale_w(2, 3, 0)
         norm(1, 0, 4)
         rescale(1, 0, 4)
         weigh(2, 1)
         scores(3, 1)
         weigh(2, 2)
         scores(3, 2)
-        weigh(2, 3)
-        scores(3, 3)
         weigh(3, 0)
+        weigh(3, 1)
         quant_w(2, 0, 4)
         values(2, 0, 4)
+        quant_w(3, 0, 2)
+        values(3, 0, 2)
         gain(1, 0, 4)
         store(1, 0, 4)
         norm(2, 0, 4)
-        weigh(3, 1)
-        weigh(3, 2)
-        quant_w(3, 0, 2)
-        values(3, 0, 2)
         norm(3, 0, 2)
+        weigh(3, 2)
         weigh(3, 3)
         quant_w(3, 2, 3)
         values(3, 2, 3)
         quant_w(3, 3, 4)
         values(3, 3, 4)
-        norm(3, 2, 3)
-        norm(3, 3, 4)
+        norm(3, 2, 4)
         finish(2, 0, 4)
         store(2, 0, 4)
         finish(3, 0, 2)

@@ -16,6 +16,11 @@ PACK = 4
 ROWS = D // PACK
 QT = 128
 TILES = NQ // QT
+W_COLS = QT * PACK
+SHARED_HEAD = H - 1
+K_SPLIT = 32
+Q_SPLIT = 64
+EPS = 256.0 * 1e-5
 FLOPS = 2 * H * NQ * N * (D + E)
 
 
@@ -26,126 +31,84 @@ def tile_rows_a_relu_onorm_kernel(tc, qT, kT, t, v, gn, out):
         ps = ctx.enter_context(tc.psum_pool(name="ps", bufs=1))
         ctx.enter_context(tc.manual_schedule())
 
-        def tiles(name, count, shape, dtype):
-            return [sb.tile(shape, dtype, name="%s%d" % (name, i), align_bytes=64) for i in range(count)]
+        def tiles(name, shapes, dtype):
+            return [sb.tile(shape, dtype, name="%s%d" % (name, n), align_bytes=64) for n, shape in enumerate(shapes)]
 
-        k_raw = sb.tile([P, PACK, N], F32)
-        q_raw0 = sb.tile([P, PACK, 2 * QT], F32)
-        q_raw1 = sb.tile([P, PACK, 2 * QT], F32)
-        v_raw = tiles("v_raw", 2, [P, 2, PACK, E], F32)
         t_sb = sb.tile([P, PACK], F32)
+        k_raw = sb.tile([P, PACK, N], F32)
+        q_raw = tiles("q_raw", [[P, PACK, 2 * QT]] * 2, F32)
+        v_raw = tiles("v_raw", [[P, 2, PACK, E]] * 2, F32)
         gn_sb = sb.tile([P, E], F32)
 
-        k_bf = tiles("k_bf", 2, [P, 2, P, PACK], BF16)
-        k_codes = tiles("k_codes", 2, [P, 2 * P], U32)
-        k_scales = tiles("k_scales", 2, [P, 2 * P], U8)
+        k_bf = tiles("k_bf", [[P, 2, P, PACK]] * 2, BF16)
+        k_codes = tiles("k_codes", [[P, 2 * P]] * 2, U32)
+        k_scales = tiles("k_scales", [[P, 2 * P]] * 2, U8)
         q_widths = [QT, QT, 2 * QT]
-        q_codes = [sb.tile([P, w], U32, name="q_codes%d" % i, align_bytes=64) for i, w in enumerate(q_widths)]
-        q_scales = [sb.tile([P, w], U8, name="q_scales%d" % i, align_bytes=64) for i, w in enumerate(q_widths)]
-        q_bf0 = sb.tile([P, QT * PACK], BF16, align_bytes=64)
+        q_bf = tiles("q_bf", [[P, width * PACK] for width in q_widths], BF16)
+        q_codes = tiles("q_codes", [[P, width] for width in q_widths], U32)
+        q_scales = tiles("q_scales", [[P, width] for width in q_widths], U8)
         v_bf = sb.tile([P, H * E * PACK], BF16, align_bytes=64)
         v_codes = sb.tile([P, H * E], U32, align_bytes=64)
         v_scales = sb.tile([P, H * E], U8, align_bytes=64)
-        w_bf = {}
-        w_plan = [[(0, 4, "w0")], [(0, 4, "slot_a")], [(0, 4, "w2")], [(0, 2, "slot_b"), (2, 4, "w3")]]
-        res_tags = ["slot_a", "slot_b", "res2", "res3"]
-        res = {}
-        scaled = tiles("scaled", TILES, [P, H, E], F32)
-        w_codes = tiles("w_codes", TILES, [P, H * QT], U32)
-        w_scales = tiles("w_scales", TILES, [P, H * QT], U8)
-        relu_sb = tiles("relu_sb", TILES, [P, 2, QT * PACK], F32)
-        squares = tiles("squares", TILES, [P, H, E], BF16)
-        sums = tiles("sums", TILES, [P, H], F32)
-        inv = tiles("inv", TILES, [P, H], F32)
+
+        t_full = sb.tile([P, W_COLS], F32, align_bytes=64)
+        w_codes = tiles("w_codes", [[P, H * QT]] * TILES, U32)
+        w_scales = tiles("w_scales", [[P, H * QT]] * TILES, U8)
+        relu_sb = tiles("relu_sb", [[P, W_COLS]] * 2, F32)
+        normed = tiles("normed", [[P, H, E]] * 2, F32)
+        squares = tiles("squares", [[P, H, E]] * TILES, BF16)
+        sums = tiles("sums", [[P, H]] * TILES, F32)
+        inv_rms = tiles("inv_rms", [[P, H]] * TILES, F32)
+
         score = [ps.tile([P, PACK, QT], F32, name="score%d" % g) for g in range(H)]
-        y_banks = [ps.tile([P, H, E], F32, name="y%d" % g) for g in range(TILES)]
+        y_banks = [ps.tile([P, H, E], F32, name="y%d" % b) for b in range(TILES)]
+
+        y_bank_of = [[0, 0, 1, 1], [2, 2, 3, 3], [0, 0, 0, 0], [1, 2, 3, 3]]
 
         def y(c, g):
-            bank = (2 * c + g // 2) % TILES
-            return y_banks[bank][:, g, :]
+            return y_banks[y_bank_of[c][g]][:, g, :]
+
+        w_bf = {}
+        result = {}
+
+        def new_weights(c, g0, g1, tag):
+            piece = sb.tile([P, (g1 - g0) * W_COLS], BF16, name="w_bf%d_%d" % (c, g0), tag=tag, align_bytes=64)
+            for g in range(g0, g1):
+                w_bf[(c, g)] = (piece, g0)
+
+        def new_result(c, tag):
+            result[c] = sb.tile([P, H, E], F32, name="result%d" % c, tag=tag, align_bytes=64)
 
         def w_cols(c, g0, g1):
-            for first, last, tag in w_plan[c]:
-                if first <= g0 and g1 <= last:
-                    if (c, first) not in w_bf:
-                        w_bf.setdefault((c, first), sb.tile([P, (last - first) * QT * PACK], BF16, name="w_%d_%d" % (c, first), tag=tag, align_bytes=64))
-                    return w_bf[(c, first)][:, (g0 - first) * QT * PACK : (g1 - first) * QT * PACK]
-            raise ValueError("no such piece")
-
-        def result(c):
-            if c not in res:
-                res.setdefault(c, sb.tile([P, H, E], F32, name="res%d" % c, tag=res_tags[c], align_bytes=64))
-            return res[c]
-
-        q_bf = [q_bf0[:], v_bf[:, 0 : QT * PACK], w_cols(1, 2, 4)]
-        q_view = qT.rearrange("h (p j) n -> (h p) j n", j=PACK)
-        k_view = kT.rearrange("h (p j) n -> (h p) j n", j=PACK)
-        v_view = v.rearrange("h (p j) e -> p h (j e)", j=PACK)
-        out_view = out.rearrange("h q e -> q h e")
+            piece, first = w_bf[(c, g0)]
+            return piece[:, (g0 - first) * W_COLS : (g1 - first) * W_COLS]
 
         def quantize(codes, scales, src):
             nc.vector.quantize_mx(out=codes.bitcast(FP8X4), scales=scales, in_=src)
 
-        def load_k():
-            nc.sync.dma_start(out=k_raw[:], in_=k_view)
+        def round_k(copy, half, s0, s1):
+            src = k_raw[:].rearrange("p j (s r) -> p s j r", r=PACK)[:, s0:s1, :, 2 * half : 2 * half + 2]
+            copy(out=k_bf[half][:].rearrange("p r s j -> p s j r")[:, s0:s1, :, :], in_=src)
 
-        def load_qa():
-            nc.sync.dma_start(out=q_raw0[:], in_=q_view[:, :, 0 : 2 * QT])
+        def quantize_k(half):
+            quantize(k_codes[half][:], k_scales[half][:], k_bf[half][:].rearrange("p r s j -> p (r s j)"))
 
-        def load_qb():
-            nc.sync.dma_start(out=q_raw1[:], in_=q_view[:, :, 2 * QT : NQ])
-
-        def load_t():
-            nc.sync.dma_start(out=t_sb[:], in_=t.rearrange("(p j) o -> p (j o)", j=PACK))
-
-        def load_v(i):
-            nc.sync.dma_start(out=v_raw[i][:].rearrange("p h j e -> p h (j e)"), in_=v_view[:, 2 * i : 2 * i + 2, :])
-
-        def load_gn():
-            nc.sync.dma_start(out=gn_sb[:], in_=gn)
-
-        def warm():
-            one = sb.tile([P, 1], F32)
-            warm_out = sb.tile([P, 1], F32)
-            nc.gpsimd.memset(one[:], 1.0)
-            nc.scalar.activation(out=warm_out[:], in_=one[:], func=ACT.Abs_reciprocal_sqrt)
-
-        def gcopy(out, in_):
-            nc.gpsimd.tensor_scalar(out=out, in0=in_, scalar1=1.0, scalar2=0.0, op0=ALU.mult, op1=ALU.add)
-
-        def cast_kp(copy, i, s0, s1):
-            src = k_raw[:].rearrange("p j (s r) -> p s j r", r=PACK)[:, s0:s1, :, 2 * i : 2 * i + 2]
-            copy(out=k_bf[i][:].rearrange("p r s j -> p s j r")[:, s0:s1, :, :], in_=src)
-
-        def quant_kp(i):
-            quantize(k_codes[i][:], k_scales[i][:], k_bf[i][:].rearrange("p r s j -> p (r s j)"))
-
-        def cast_qp(copy, i, n0, n1):
-            raw = [q_raw0[:, :, 0:QT], q_raw0[:, :, QT : 2 * QT], q_raw1[:]][i]
+        def round_q(copy, piece, n0, n1):
+            raw = [q_raw[0][:, :, 0:QT], q_raw[0][:, :, QT : 2 * QT], q_raw[1][:]][piece]
             copy(
-                out=q_bf[i][:, n0 * PACK : n1 * PACK].rearrange("p (c i j) -> p c j i", i=PACK, j=PACK),
-                in_=raw[:, :, n0:n1].rearrange("p j (c i) -> p c j i", i=PACK),
+                out=q_bf[piece][:, n0 * PACK : n1 * PACK].rearrange("p (n x j) -> p n j x", x=PACK, j=PACK),
+                in_=raw[:, :, n0:n1].rearrange("p j (n x) -> p n j x", x=PACK),
             )
 
-        def quant_qp(i):
-            quantize(q_codes[i][:], q_scales[i][:], q_bf[i])
+        def quantize_q(piece):
+            quantize(q_codes[piece][:], q_scales[piece][:], q_bf[piece][:])
 
-        def cast_v(copy, i):
-            half = v_bf[:, i * 2 * E * PACK : (i + 1) * 2 * E * PACK]
-            if copy is gcopy:
-                copy(out=half.rearrange("p (h e j) -> p h e j", h=2, j=PACK), in_=v_raw[i][:].rearrange("p h j e -> p h e j"))
-            else:
-                copy(
-                    out=half.rearrange("p (h c i j) -> p h c j i", h=2, i=PACK, j=PACK),
-                    in_=v_raw[i][:].rearrange("p h j (c i) -> p h c j i", i=PACK),
-                )
-
-        def quant_v_all():
-            quantize(v_codes[:], v_scales[:], v_bf[:])
-
-        def scores(c, g):
-            scores_half(c, g, 0)
-            scores_half(c, g, 1)
+        def round_v(pair):
+            dst = v_bf[:, pair * 2 * E * PACK : (pair + 1) * 2 * E * PACK]
+            nc.scalar.copy(
+                out=dst.rearrange("p (h n x r) -> p h n r x", h=2, x=PACK, r=PACK),
+                in_=v_raw[pair][:].rearrange("p h r (n x) -> p h n r x", x=PACK),
+            )
 
         def scores_half(c, g, half):
             rows = slice(ROWS * g, ROWS * (g + 1))
@@ -155,205 +118,215 @@ def tile_rows_a_relu_onorm_kernel(tc, qT, kT, t, v, gn, out):
                 k_cols = slice(P * (r % 2), P * (r % 2 + 1))
                 nc.tensor.matmul_mx(
                     out=score[g][:, r, :],
-                    lhsT=k_codes[r // 2][rows, k_cols].bitcast(FP8X4),
-                    lhsT_scale=k_scales[r // 2][rows, k_cols],
+                    lhsT=k_codes[half][rows, k_cols].bitcast(FP8X4),
+                    lhsT_scale=k_scales[half][rows, k_cols],
                     rhs=q_codes[piece][rows, q_cols].bitcast(FP8X4),
                     rhs_scale=q_scales[piece][rows, q_cols],
                     start=True,
                     stop=True,
                 )
 
-        def w_slot(c, g):
-            return w_cols(c, g, g + 1).rearrange("p (q r) -> p q r", r=PACK)
-
-        t_wide = t_sb[:, 0:PACK].unsqueeze(1).to_broadcast([P, QT, PACK])
+        def scores(c, g):
+            scores_half(c, g, 0)
+            scores_half(c, g, 1)
 
         def weigh(c, g):
             nc.vector.scalar_tensor_tensor(
-                out=w_slot(c, g),
+                out=w_cols(c, g, g + 1).rearrange("p (q r) -> p q r", r=PACK),
                 in0=score[g][:].rearrange("p r q -> p q r"),
                 scalar=0.0,
-                in1=t_wide,
+                in1=t_full[:].rearrange("p (q r) -> p q r", r=PACK),
                 op0=ALU.max,
                 op1=ALU.mult,
             )
 
-        def relu(c, g, slot):
+        def relu(c):
             nc.scalar.activation(
-                out=relu_sb[c][:, slot, :].rearrange("p (q r) -> p q r", r=PACK),
-                in_=score[g][:].rearrange("p r q -> p q r"),
+                out=relu_sb[c][:].rearrange("p (q r) -> p q r", r=PACK),
+                in_=score[SHARED_HEAD][:].rearrange("p r q -> p q r"),
                 func=ACT.Relu,
             )
 
-        def scale_w(c, g, slot):
+        def times_t(c):
             nc.gpsimd.tensor_tensor(
-                out=w_slot(c, g),
-                in0=relu_sb[c][:, slot, :].rearrange("p (q r) -> p q r", r=PACK),
-                in1=t_wide,
-                op=ALU.mult,
+                out=w_cols(c, SHARED_HEAD, SHARED_HEAD + 1), in0=relu_sb[c][:], in1=t_full[:], op=ALU.mult
             )
 
-        def quant_w(c, g0, g1):
-            quantize(
-                w_codes[c][:, g0 * QT : g1 * QT],
-                w_scales[c][:, g0 * QT : g1 * QT],
-                w_cols(c, g0, g1),
-            )
-
-        def value(c, g):
-            w_span = slice(g * QT, (g + 1) * QT)
-            v_cols = slice(g * E, (g + 1) * E)
-            nc.tensor.matmul_mx(
-                out=y(c, g),
-                lhsT=w_codes[c][:, w_span].bitcast(FP8X4),
-                lhsT_scale=w_scales[c][:, w_span],
-                rhs=v_codes[:, v_cols].bitcast(FP8X4),
-                rhs_scale=v_scales[:, v_cols],
-                start=True,
-                stop=True,
-            )
-
-        def square(c, g):
-            nc.scalar.activation(
-                out=squares[c][:, g, :], in_=y(c, g), func=ACT.Square, accum_out=sums[c][:, g : g + 1]
-            )
-
-        def root(c, g0, g1):
-            nc.scalar.activation(
-                out=inv[c][:, g0:g1],
-                in_=sums[c][:, g0:g1],
-                func=ACT.Abs_reciprocal_sqrt,
-                scale=1.0 / E,
-                bias=256.0 * 1e-5,
-            )
-
-        def finish_one(c, g):
-            nc.vector.scalar_tensor_tensor(
-                out=result(c)[:, g, :],
-                in0=y(c, g),
-                scalar=inv[c][:, g : g + 1],
-                in1=gn_sb[:],
-                op0=ALU.mult,
-                op1=ALU.mult,
-            )
-
-        def store(c, g0, g1):
-            nc.sync.dma_start(out=out_view[c * QT : (c + 1) * QT, g0:g1, :], in_=result(c)[:, g0:g1, :])
+        def quantize_w(c, g0, g1):
+            quantize(w_codes[c][:, g0 * QT : g1 * QT], w_scales[c][:, g0 * QT : g1 * QT], w_cols(c, g0, g1))
 
         def values(c, g0, g1):
             for g in range(g0, g1):
-                value(c, g)
+                w_span = slice(g * QT, (g + 1) * QT)
+                v_span = slice(g * E, (g + 1) * E)
+                nc.tensor.matmul_mx(
+                    out=y(c, g),
+                    lhsT=w_codes[c][:, w_span].bitcast(FP8X4),
+                    lhsT_scale=w_scales[c][:, w_span],
+                    rhs=v_codes[:, v_span].bitcast(FP8X4),
+                    rhs_scale=v_scales[:, v_span],
+                    start=True,
+                    stop=True,
+                )
 
-        def rescale(c, g0, g1):
+        def sum_squares(c, g0, g1):
             for g in range(g0, g1):
-                nc.scalar.activation(out=scaled[c][:, g, :], in_=y(c, g), func=ACT.Copy, scale=inv[c][:, g : g + 1])
+                nc.scalar.activation(
+                    out=squares[c][:, g, :], in_=y(c, g), func=ACT.Square, accum_out=sums[c][:, g : g + 1]
+                )
 
-        def gain(c, g0, g1):
-            nc.gpsimd.tensor_tensor(
-                out=result(c)[:, g0:g1, :],
-                in0=scaled[c][:, g0:g1, :],
-                in1=gn_sb[:].unsqueeze(1).to_broadcast([P, g1 - g0, E]),
-                op=ALU.mult,
+        def root(c, g0, g1):
+            nc.scalar.activation(
+                out=inv_rms[c][:, g0:g1],
+                in_=sums[c][:, g0:g1],
+                func=ACT.Abs_reciprocal_sqrt,
+                scale=1.0 / E,
+                bias=EPS,
             )
 
-        def norm(c, g0, g1):
-            for g in range(g0, g1):
-                square(c, g)
-            root(c, g0, g1)
+        def store(c, g0, g1):
+            dst = out.rearrange("h q e -> q h e")[c * QT : (c + 1) * QT, g0:g1, :]
+            nc.sync.dma_start(out=dst, in_=result[c][:, g0:g1, :])
+
+        def normalise(c):
+            sum_squares(c, 0, H)
+            root(c, 0, H)
+            for g in range(H):
+                nc.scalar.activation(
+                    out=normed[c][:, g, :], in_=y(c, g), func=ACT.Copy, scale=inv_rms[c][:, g : g + 1]
+                )
+
+        def apply_gain(c):
+            nc.gpsimd.tensor_tensor(
+                out=result[c][:],
+                in0=normed[c][:],
+                in1=gn_sb[:].unsqueeze(1).to_broadcast([P, H, E]),
+                op=ALU.mult,
+            )
+            store(c, 0, H)
 
         def finish(c, g0, g1):
             for g in range(g0, g1):
-                finish_one(c, g)
+                nc.vector.scalar_tensor_tensor(
+                    out=result[c][:, g, :],
+                    in0=y(c, g),
+                    scalar=inv_rms[c][:, g : g + 1],
+                    in1=gn_sb[:],
+                    op0=ALU.mult,
+                    op1=ALU.mult,
+                )
+            store(c, g0, g1)
 
-        vcopy = nc.vector.tensor_copy
-        scopy = nc.scalar.copy
+        q_view = qT.rearrange("h (p j) n -> (h p) j n", j=PACK)
+        v_view = v.rearrange("h (s r) e -> s h (r e)", r=PACK)
+        nc.sync.dma_start(out=t_sb[:], in_=t.rearrange("(s r) o -> s (r o)", r=PACK))
+        nc.sync.dma_start(out=k_raw[:], in_=kT.rearrange("h (p j) n -> (h p) j n", j=PACK))
+        nc.sync.dma_start(out=q_raw[0][:], in_=q_view[:, :, 0 : 2 * QT])
+        for pair in range(2):
+            nc.sync.dma_start(
+                out=v_raw[pair][:].rearrange("p h r e -> p h (r e)"), in_=v_view[:, 2 * pair : 2 * pair + 2, :]
+            )
+        nc.sync.dma_start(out=q_raw[1][:], in_=q_view[:, :, 2 * QT : NQ])
+        nc.sync.dma_start(out=gn_sb[:], in_=gn)
 
-        load_k()
-        load_qa()
-        load_t()
-        load_v(0)
-        load_v(1)
-        load_qb()
-        load_gn()
-        warm()
-        cast_kp(vcopy, 0, 0, 128)
-        cast_kp(vcopy, 1, 0, 32)
-        cast_kp(scopy, 1, 32, 128)
-        quant_kp(0)
-        cast_qp(vcopy, 0, 0, 64)
-        cast_qp(scopy, 0, 64, 128)
-        quant_qp(0)
+        one = sb.tile([P, 1], F32)
+        warm_out = sb.tile([P, 1], F32)
+        nc.gpsimd.memset(one[:], 1.0)
+        nc.scalar.activation(out=warm_out[:], in_=one[:], func=ACT.Abs_reciprocal_sqrt)
+
+        nc.vector.tensor_copy(
+            out=t_full[:].rearrange("p (q r) -> p q r", r=PACK),
+            in_=t_sb[:].unsqueeze(1).to_broadcast([P, QT, PACK]),
+        )
+
+        round_k(nc.vector.tensor_copy, 0, 0, P)
+        round_k(nc.vector.tensor_copy, 1, 0, K_SPLIT)
+        round_k(nc.scalar.copy, 1, K_SPLIT, P)
+        quantize_k(0)
+        round_q(nc.vector.tensor_copy, 0, 0, Q_SPLIT)
+        round_q(nc.scalar.copy, 0, Q_SPLIT, QT)
+        quantize_q(0)
         scores_half(0, 0, 0)
-        scores_half(0, 3, 0)
-        quant_kp(1)
+        scores_half(0, SHARED_HEAD, 0)
+        quantize_k(1)
         scores_half(0, 0, 1)
-        scores_half(0, 3, 1)
+        scores_half(0, SHARED_HEAD, 1)
         scores(0, 1)
         scores(0, 2)
-        cast_qp(scopy, 1, 0, 128)
-        quant_qp(1)
-        cast_v(gcopy, 0)
+        round_q(nc.scalar.copy, 1, 0, QT)
+        quantize_q(1)
+        round_v(0)
+
+
+        new_weights(0, 0, H, "early")
         weigh(0, 0)
         scores(1, 0)
-        relu(0, 3, 0)
-        scores(1, 3)
-        scale_w(0, 3, 0)
-        weigh(0, 1)
-        scores(1, 1)
-        weigh(0, 2)
-        scores(1, 2)
-        cast_v(scopy, 1)
-        cast_qp(scopy, 2, 0, 256)
-        relu(1, 3, 0)
+        relu(0)
+        times_t(0)
+        scores(1, SHARED_HEAD)
+        for g in (1, 2):
+            weigh(0, g)
+            scores(1, g)
+        round_v(1)
+        round_q(nc.scalar.copy, 2, 0, 2 * QT)
+        relu(1)
+        new_weights(1, 0, 2, "w_bf1")
         weigh(1, 0)
-        quant_v_all()
-        quant_w(0, 0, 4)
-        values(0, 0, 4)
-        quant_qp(2)
-        scores(2, 0)
-        scores(2, 3)
-        scale_w(1, 3, 0)
-        norm(0, 0, 4)
-        rescale(0, 0, 4)
         weigh(1, 1)
-        scores(2, 1)
+        quantize(v_codes[:], v_scales[:], v_bf[:])
+        quantize_q(2)
+        for g in (0, 1, SHARED_HEAD):
+            scores(2, g)
+        quantize_w(0, 0, H)
+        values(0, 0, H)
+
+        new_weights(1, 2, H, "early")
+        times_t(1)
+        normalise(0)
         weigh(1, 2)
         scores(2, 2)
-        weigh(2, 0)
-        scores(3, 0)
-        quant_w(1, 0, 4)
-        values(1, 0, 4)
-        gain(0, 0, 4)
-        store(0, 0, 4)
-        relu(2, 3, 0)
-        scores(3, 3)
-        scale_w(2, 3, 0)
-        norm(1, 0, 4)
-        rescale(1, 0, 4)
-        weigh(2, 1)
-        scores(3, 1)
-        weigh(2, 2)
-        scores(3, 2)
+        new_weights(2, 0, H, "w_bf2")
+        for g in (0, 1):
+            weigh(2, g)
+            scores(3, g)
+        quantize_w(1, 0, 2)
+        quantize_w(1, 2, H)
+        values(1, 0, H)
+
+        new_result(0, "early")
+        apply_gain(0)
+        normalise(1)
+        for g in (2, 3):
+            weigh(2, g)
+            scores(3, g)
+        new_weights(3, 0, 1, "late")
         weigh(3, 0)
-        weigh(3, 1)
-        quant_w(2, 0, 4)
-        values(2, 0, 4)
-        quant_w(3, 0, 2)
-        values(3, 0, 2)
-        gain(1, 0, 4)
-        store(1, 0, 4)
-        norm(2, 0, 4)
-        norm(3, 0, 2)
-        weigh(3, 2)
-        weigh(3, 3)
-        quant_w(3, 2, 3)
-        values(3, 2, 3)
-        quant_w(3, 3, 4)
-        values(3, 3, 4)
-        norm(3, 2, 4)
-        finish(2, 0, 4)
-        store(2, 0, 4)
+        quantize_w(2, 0, H)
+        values(2, 0, H)
+        quantize_w(3, 0, 1)
+        values(3, 0, 1)
+
+        new_result(1, "late")
+        apply_gain(1)
+        sum_squares(2, 0, H)
+        root(2, 0, H)
+        sum_squares(3, 0, 1)
+        root(3, 0, 1)
+        new_weights(3, 1, H, "w_bf3")
+        for g in range(1, H):
+            weigh(3, g)
+
+        for g in range(1, H):
+            quantize_w(3, g, g + 1)
+            values(3, g, g + 1)
+        sum_squares(3, 1, 3)
+        root(3, 1, 2)
+        sum_squares(3, 3, H)
+        root(3, 2, H)
+        new_result(2, "result2")
+        finish(2, 0, 2)
+        finish(2, 2, H)
+        new_result(3, "result3")
         finish(3, 0, 2)
-        store(3, 0, 2)
-        finish(3, 2, 4)
-        store(3, 2, 4)
+        finish(3, 2, 3)
+        finish(3, 3, H)

from contextlib import ExitStack

import concourse.mybir as mybir

F32 = mybir.dt.float32
BF16 = mybir.dt.bfloat16
U32 = mybir.dt.uint32
U8 = mybir.dt.uint8
FP8X4 = mybir.dt.float8_e4m3fn_x4
ACT = mybir.ActivationFunctionType
ALU = mybir.AluOpType

H, D, NQ, N, E = 4, 128, 512, 512, 128
P = 128
PACK = 4
ROWS = D // PACK
QT = 128
TILES = NQ // QT
W_COLS = QT * PACK
SHARED_HEAD = H - 1
K_SPLIT = 32
Q_SPLIT = 64
EPS = 256.0 * 1e-5
FLOPS = 2 * H * NQ * N * (D + E)


def tile_rows_a_relu_onorm_kernel(tc, qT, kT, t, v, gn, out):
    nc = tc.nc
    with ExitStack() as ctx:
        sb = ctx.enter_context(tc.tile_pool(name="sb", bufs=1))
        ps = ctx.enter_context(tc.psum_pool(name="ps", bufs=1))
        ctx.enter_context(tc.manual_schedule())

        def tiles(name, shapes, dtype):
            return [sb.tile(shape, dtype, name="%s%d" % (name, n), align_bytes=64) for n, shape in enumerate(shapes)]

        t_sb = sb.tile([P, PACK], F32)
        k_raw = sb.tile([P, PACK, N], F32)
        q_raw = tiles("q_raw", [[P, PACK, 2 * QT]] * 2, F32)
        v_raw = tiles("v_raw", [[P, 2, PACK, E]] * 2, F32)
        gn_sb = sb.tile([P, E], F32)

        k_bf = tiles("k_bf", [[P, 2, P, PACK]] * 2, BF16)
        k_codes = tiles("k_codes", [[P, 2 * P]] * 2, U32)
        k_scales = tiles("k_scales", [[P, 2 * P]] * 2, U8)
        q_widths = [QT, QT, 2 * QT]
        q_bf = tiles("q_bf", [[P, width * PACK] for width in q_widths], BF16)
        q_codes = tiles("q_codes", [[P, width] for width in q_widths], U32)
        q_scales = tiles("q_scales", [[P, width] for width in q_widths], U8)
        v_bf = sb.tile([P, H * E * PACK], BF16, align_bytes=64)
        v_codes = sb.tile([P, H * E], U32, align_bytes=64)
        v_scales = sb.tile([P, H * E], U8, align_bytes=64)

        t_full = sb.tile([P, W_COLS], F32, align_bytes=64)
        w_codes = tiles("w_codes", [[P, H * QT]] * TILES, U32)
        w_scales = tiles("w_scales", [[P, H * QT]] * TILES, U8)
        relu_sb = tiles("relu_sb", [[P, W_COLS]] * 2, F32)
        normed = tiles("normed", [[P, H, E]] * 2, F32)
        squares = tiles("squares", [[P, H, E]] * TILES, BF16)
        sums = tiles("sums", [[P, H]] * TILES, F32)
        inv_rms = tiles("inv_rms", [[P, H]] * TILES, F32)

        score = [ps.tile([P, PACK, QT], F32, name="score%d" % g) for g in range(H)]
        y_banks = [ps.tile([P, H, E], F32, name="y%d" % b) for b in range(TILES)]

        y_bank_of = [[0, 0, 1, 1], [2, 2, 3, 3], [0, 0, 0, 0], [1, 2, 3, 3]]

        def y(c, g):
            return y_banks[y_bank_of[c][g]][:, g, :]

        w_bf = {}
        result = {}

        def new_weights(c, g0, g1, tag):
            piece = sb.tile([P, (g1 - g0) * W_COLS], BF16, name="w_bf%d_%d" % (c, g0), tag=tag, align_bytes=64)
            for g in range(g0, g1):
                w_bf[(c, g)] = (piece, g0)

        def new_result(c, tag):
            result[c] = sb.tile([P, H, E], F32, name="result%d" % c, tag=tag, align_bytes=64)

        def w_cols(c, g0, g1):
            piece, first = w_bf[(c, g0)]
            return piece[:, (g0 - first) * W_COLS : (g1 - first) * W_COLS]

        def quantize(codes, scales, src):
            nc.vector.quantize_mx(out=codes.bitcast(FP8X4), scales=scales, in_=src)

        def round_k(copy, half, s0, s1):
            src = k_raw[:].rearrange("p j (s r) -> p s j r", r=PACK)[:, s0:s1, :, 2 * half : 2 * half + 2]
            copy(out=k_bf[half][:].rearrange("p r s j -> p s j r")[:, s0:s1, :, :], in_=src)

        def quantize_k(half):
            quantize(k_codes[half][:], k_scales[half][:], k_bf[half][:].rearrange("p r s j -> p (r s j)"))

        def round_q(copy, piece, n0, n1):
            raw = [q_raw[0][:, :, 0:QT], q_raw[0][:, :, QT : 2 * QT], q_raw[1][:]][piece]
            copy(
                out=q_bf[piece][:, n0 * PACK : n1 * PACK].rearrange("p (n x j) -> p n j x", x=PACK, j=PACK),
                in_=raw[:, :, n0:n1].rearrange("p j (n x) -> p n j x", x=PACK),
            )

        def quantize_q(piece):
            quantize(q_codes[piece][:], q_scales[piece][:], q_bf[piece][:])

        def round_v(pair):
            dst = v_bf[:, pair * 2 * E * PACK : (pair + 1) * 2 * E * PACK]
            nc.scalar.copy(
                out=dst.rearrange("p (h n x r) -> p h n r x", h=2, x=PACK, r=PACK),
                in_=v_raw[pair][:].rearrange("p h r (n x) -> p h n r x", x=PACK),
            )

        def scores_half(c, g, half):
            rows = slice(ROWS * g, ROWS * (g + 1))
            piece = min(c, 2)
            q_cols = slice(QT * (c - piece), QT * (c - piece + 1))
            for r in range(2 * half, 2 * half + 2):
                k_cols = slice(P * (r % 2), P * (r % 2 + 1))
                nc.tensor.matmul_mx(
                    out=score[g][:, r, :],
                    lhsT=k_codes[half][rows, k_cols].bitcast(FP8X4),
                    lhsT_scale=k_scales[half][rows, k_cols],
                    rhs=q_codes[piece][rows, q_cols].bitcast(FP8X4),
                    rhs_scale=q_scales[piece][rows, q_cols],
                    start=True,
                    stop=True,
                )

        def scores(c, g):
            scores_half(c, g, 0)
            scores_half(c, g, 1)

        def weigh(c, g):
            nc.vector.scalar_tensor_tensor(
                out=w_cols(c, g, g + 1).rearrange("p (q r) -> p q r", r=PACK),
                in0=score[g][:].rearrange("p r q -> p q r"),
                scalar=0.0,
                in1=t_full[:].rearrange("p (q r) -> p q r", r=PACK),
                op0=ALU.max,
                op1=ALU.mult,
            )

        def relu(c):
            nc.scalar.activation(
                out=relu_sb[c][:].rearrange("p (q r) -> p q r", r=PACK),
                in_=score[SHARED_HEAD][:].rearrange("p r q -> p q r"),
                func=ACT.Relu,
            )

        def times_t(c):
            nc.gpsimd.tensor_tensor(
                out=w_cols(c, SHARED_HEAD, SHARED_HEAD + 1), in0=relu_sb[c][:], in1=t_full[:], op=ALU.mult
            )

        def quantize_w(c, g0, g1):
            quantize(w_codes[c][:, g0 * QT : g1 * QT], w_scales[c][:, g0 * QT : g1 * QT], w_cols(c, g0, g1))

        def values(c, g0, g1):
            for g in range(g0, g1):
                w_span = slice(g * QT, (g + 1) * QT)
                v_span = slice(g * E, (g + 1) * E)
                nc.tensor.matmul_mx(
                    out=y(c, g),
                    lhsT=w_codes[c][:, w_span].bitcast(FP8X4),
                    lhsT_scale=w_scales[c][:, w_span],
                    rhs=v_codes[:, v_span].bitcast(FP8X4),
                    rhs_scale=v_scales[:, v_span],
                    start=True,
                    stop=True,
                )

        def sum_squares(c, g0, g1):
            for g in range(g0, g1):
                nc.scalar.activation(
                    out=squares[c][:, g, :], in_=y(c, g), func=ACT.Square, accum_out=sums[c][:, g : g + 1]
                )

        def root(c, g0, g1):
            nc.scalar.activation(
                out=inv_rms[c][:, g0:g1],
                in_=sums[c][:, g0:g1],
                func=ACT.Abs_reciprocal_sqrt,
                scale=1.0 / E,
                bias=EPS,
            )

        def store(c, g0, g1):
            dst = out.rearrange("h q e -> q h e")[c * QT : (c + 1) * QT, g0:g1, :]
            nc.sync.dma_start(out=dst, in_=result[c][:, g0:g1, :])

        def normalise(c):
            sum_squares(c, 0, H)
            root(c, 0, H)
            for g in range(H):
                nc.scalar.activation(
                    out=normed[c][:, g, :], in_=y(c, g), func=ACT.Copy, scale=inv_rms[c][:, g : g + 1]
                )

        def apply_gain(c):
            nc.gpsimd.tensor_tensor(
                out=result[c][:],
                in0=normed[c][:],
                in1=gn_sb[:].unsqueeze(1).to_broadcast([P, H, E]),
                op=ALU.mult,
            )
            store(c, 0, H)

        def finish(c, g0, g1):
            for g in range(g0, g1):
                nc.vector.scalar_tensor_tensor(
                    out=result[c][:, g, :],
                    in0=y(c, g),
                    scalar=inv_rms[c][:, g : g + 1],
                    in1=gn_sb[:],
                    op0=ALU.mult,
                    op1=ALU.mult,
                )
            store(c, g0, g1)

        q_view = qT.rearrange("h (p j) n -> (h p) j n", j=PACK)
        v_view = v.rearrange("h (s r) e -> s h (r e)", r=PACK)
        nc.sync.dma_start(out=t_sb[:], in_=t.rearrange("(s r) o -> s (r o)", r=PACK))
        nc.sync.dma_start(out=k_raw[:], in_=kT.rearrange("h (p j) n -> (h p) j n", j=PACK))
        nc.sync.dma_start(out=q_raw[0][:], in_=q_view[:, :, 0 : 2 * QT])
        for pair in range(2):
            nc.sync.dma_start(
                out=v_raw[pair][:].rearrange("p h r e -> p h (r e)"), in_=v_view[:, 2 * pair : 2 * pair + 2, :]
            )
        nc.sync.dma_start(out=q_raw[1][:], in_=q_view[:, :, 2 * QT : NQ])
        nc.sync.dma_start(out=gn_sb[:], in_=gn)

        one = sb.tile([P, 1], F32)
        warm_out = sb.tile([P, 1], F32)
        nc.gpsimd.memset(one[:], 1.0)
        nc.scalar.activation(out=warm_out[:], in_=one[:], func=ACT.Abs_reciprocal_sqrt)

        nc.vector.tensor_copy(
            out=t_full[:].rearrange("p (q r) -> p q r", r=PACK),
            in_=t_sb[:].unsqueeze(1).to_broadcast([P, QT, PACK]),
        )

        round_k(nc.vector.tensor_copy, 0, 0, P)
        round_k(nc.vector.tensor_copy, 1, 0, K_SPLIT)
        round_k(nc.scalar.copy, 1, K_SPLIT, P)
        quantize_k(0)
        round_q(nc.vector.tensor_copy, 0, 0, Q_SPLIT)
        round_q(nc.scalar.copy, 0, Q_SPLIT, QT)
        quantize_q(0)
        scores_half(0, 0, 0)
        scores_half(0, SHARED_HEAD, 0)
        quantize_k(1)
        scores_half(0, 0, 1)
        scores_half(0, SHARED_HEAD, 1)
        scores(0, 1)
        scores(0, 2)
        round_q(nc.scalar.copy, 1, 0, QT)
        quantize_q(1)
        round_v(0)


        new_weights(0, 0, H, "early")
        weigh(0, 0)
        scores(1, 0)
        relu(0)
        times_t(0)
        scores(1, SHARED_HEAD)
        for g in (1, 2):
            weigh(0, g)
            scores(1, g)
        round_v(1)
        round_q(nc.scalar.copy, 2, 0, 2 * QT)
        relu(1)
        new_weights(1, 0, 2, "w_bf1")
        weigh(1, 0)
        weigh(1, 1)
        quantize(v_codes[:], v_scales[:], v_bf[:])
        quantize_q(2)
        for g in (0, 1, SHARED_HEAD):
            scores(2, g)
        quantize_w(0, 0, H)
        values(0, 0, H)

        new_weights(1, 2, H, "early")
        times_t(1)
        normalise(0)
        weigh(1, 2)
        scores(2, 2)
        new_weights(2, 0, H, "w_bf2")
        for g in (0, 1):
            weigh(2, g)
            scores(3, g)
        quantize_w(1, 0, 2)
        quantize_w(1, 2, H)
        values(1, 0, H)

        new_result(0, "early")
        apply_gain(0)
        normalise(1)
        for g in (2, 3):
            weigh(2, g)
            scores(3, g)
        new_weights(3, 0, 1, "late")
        weigh(3, 0)
        quantize_w(2, 0, H)
        values(2, 0, H)
        quantize_w(3, 0, 1)
        values(3, 0, 1)

        new_result(1, "late")
        apply_gain(1)
        sum_squares(2, 0, H)
        root(2, 0, H)
        sum_squares(3, 0, 1)
        root(3, 0, 1)
        new_weights(3, 1, H, "w_bf3")
        for g in range(1, H):
            weigh(3, g)

        for g in range(1, H):
            quantize_w(3, g, g + 1)
            values(3, g, g + 1)
        sum_squares(3, 1, 3)
        root(3, 1, 2)
        sum_squares(3, 3, H)
        root(3, 2, H)
        new_result(2, "result2")
        finish(2, 0, 2)
        finish(2, 2, H)
        new_result(3, "result3")
        finish(3, 0, 2)
        finish(3, 2, 3)
        finish(3, 3, H)
